import numpy as np, ml_dtypes
CORES = [6,14,22,30,38,134,142,150,158]
N = 9
TK = 512
WID = [384,64,64,64,64,512,384,384,64]
def setup_inputs(rng):
    return {"x": rng.standard_normal((N, 128, TK), dtype=np.float32).astype(ml_dtypes.bfloat16), "w1": (rng.standard_normal((N, 128, 128), dtype=np.float32) / 8).astype(ml_dtypes.bfloat16), "w2": (rng.standard_normal((N, 128, 128), dtype=np.float32) / 8).astype(ml_dtypes.bfloat16)}
def setup_inputs_big(rng):
    d = setup_inputs(rng)
    for k in ("x", "w1", "w2"): d[k] = (d[k].astype(np.float32) * 1024.0).astype(d[k].dtype)
    return d
def setup_inputs_small(rng):
    d = setup_inputs(rng)
    for k in ("x", "w1", "w2"): d[k] = (d[k].astype(np.float32) * (1 / 1024.0)).astype(d[k].dtype)
    return d
def setup_inputs_apart(rng):
    d = setup_inputs(rng)
    f = (10.0 ** rng.permutation(np.linspace(-1.5, 1.5, N))).astype(np.float32).reshape(N, 1, 1)
    for k in ("x", "w1", "w2"): d[k] = (d[k].astype(np.float32) * f).astype(d[k].dtype)
    return d
def whole(x, w1, w2):
    X, W1, W2 = x.astype(np.float64), w1.astype(np.float64), w2.astype(np.float64)
    y = np.zeros((N, 128, TK))
    for r in range(N):
        for j in range(N):
            y[r] += W2[j].T @ np.maximum(W1[j].T @ X[r], 0.0)
    return {"y": y.astype(ml_dtypes.bfloat16 if x.dtype != np.float64 else np.float64)}
def reference(x, w1, w2):
    o = whole(x, w1, w2)["y"].copy()
    for r in range(N):
        o[r][:, WID[r]:] = np.nan
    return {"y": o}

@@ -1,0 +1,288 @@
+from concourse.bass import DstId, RemoteDMATransfer
+from concourse.mybir import AluOpType
+
+N = 9
+D = 128
+TK = 512
+GW = 128
+NHP = 6
+
+ALL_SITES = False
+FUSE = True
+HELP = 0
+VIA_DRAM = False
+
+SCRATCH = {
+    "wb": ("sbuf", [D, N * 2 * D], "bfloat16"),
+    "xo": ("sbuf", [D, TK], "bfloat16"),
+    "xg": ("sbuf", [D, GW], "bfloat16"),
+    "zz": ("sbuf", [D, TK], "float32"),
+    "ho": ("sbuf", [D, N * TK], "bfloat16"),
+    "hg": ("sbuf", [D, N * GW], "bfloat16"),
+    "yo": ("sbuf", [D, TK], "bfloat16"),
+    "yg": ("sbuf", [D, GW], "bfloat16"),
+    "yl": ("sbuf", [D, GW], "bfloat16"),
+    "so": ("psum", [D, TK], "float32"),
+    "sg": ("psum", [D, TK], "float32"),
+}
+for _b in range(NHP):
+    SCRATCH["hp%d" % _b] = ("psum", [D, TK], "float32")
+if VIA_DRAM:
+    SCRATCH["wd"] = ("dram", [N, D, 2 * D], "bfloat16")
+
+SEMAPHORES = ["ldw", "ldx", "xga", "zs", "sent", "yarr", "st", "fino", "fing", "cpo", "cpg"]
+SEMAPHORES += ["arr%d" % _j for _j in range(N)]
+SEMAPHORES += ["m%s%d" % (_s, _j) for _s in "og" for _j in range(N)]
+SEMAPHORES += ["r%s%d" % (_s, _j) for _s in "og" for _j in range(N)]
+if HELP:
+    SEMAPHORES += ["fw"]
+if VIA_DRAM:
+    SEMAPHORES += ["ldd"] + ["lw%d" % _j for _j in range(N)]
+
+
+def _engines(mask):
+    return [b for b in range(16) if (mask >> b) & 1]
+
+
+def _plan(T, topo):
+    wid, cores = T.tables["WID"], T.cores
+    n = len(cores)
+    wide = [r for r in range(n) if wid[r] > 2 * D]
+    narrow = [r for r in range(n) if r not in wide]
+    load = {s: wid[s] for s in wide}
+    host = {}
+    if not ALL_SITES:
+        for near in (topo.mates, topo.same_plane, lambda a, b: True):
+            for r in narrow:
+                if r in host:
+                    continue
+                cand = [s for s in wide if near(cores[r], cores[s]) and load[s] + wid[r] <= TK
+                        and load[s] - wid[s] + wid[r] <= GW]
+                if cand:
+                    s = min(cand, key=lambda q: (load[q], q))
+                    host[r] = s
+                    load[s] += wid[r]
+    sites = list(range(n)) if ALL_SITES else wide
+    guests = {s: [r for r in narrow if host.get(r) == s] for s in sites}
+    ns = len(wide)
+    free = min(range(ns), key=lambda a: (load[wide[a]] - wid[wide[a]], a))
+    order = {}
+    for j in range(n):
+        k = wide.index(j) + 1 if j in wide else narrow.index(j) + free + 1
+        order[j] = [wide[(k + w) % ns] for w in range(ns) if wide[(k + w) % ns] != j]
+        if ALL_SITES:
+            order[j] += [narrow[(j + w) % len(narrow)] for w in range(len(narrow)) if narrow[(j + w) % len(narrow)] != j]
+    helper = {}
+    if HELP:
+        nsim = topo.CORES_PER_HOST * (1 + max(topo.host(c) for c in cores))
+        for j in range(n):
+            helper[j] = min(c for c in range(nsim) if topo.host(c) == topo.host(cores[j])
+                            and topo.chip(c) == topo.chip(cores[j]) and topo.die(c) != topo.die(cores[j])
+                            and c not in cores and all(topo.may_write(c, cores[s]) for s in order[j]))
+    direct = {j: order[j][:len(order[j]) - HELP] for j in range(n)}
+    relay = {j: order[j][len(order[j]) - HELP:] for j in range(n)}
+
+    def due(j, s):
+        return direct[j].index(s) if s in direct[j] else 2 + relay[j].index(s)
+    proc = {}
+    for s in sites:
+        proc[s] = [s] + sorted([j for j in range(n) if j != s], key=lambda j: (due(j, s), j in narrow, j))
+    return sites, host, guests, direct, relay, helper, proc
+
+
+def _spread(g, core, T, topo, j, dsts, extra):
+    S, cores = T.sem, T.cores
+    blk = T.wd[j] if VIA_DRAM else T.wb[:, 2 * j * D:2 * (j + 1) * D]
+    trs, add = [], 0
+    m = 0
+    if dsts:
+        m = topo.mask(core, cores[dsts[0]])
+        for s in dsts:
+            m &= topo.mask(core, cores[s])
+    if extra is not None:
+        rid, pid = topo.addr(extra, core)
+        mx = topo.mask(core, extra) & ~m
+        trs.append(RemoteDMATransfer(dst_ids=[DstId(rid=rid, pnc=pid)], dma_engine_mask=mx, remote_sem=S.fw,
+                                     srcs=[blk], dsts=[blk]))
+        add += len(_engines(mx))
+    ids = []
+    for s in dsts:
+        rid, pid = topo.addr(cores[s], core)
+        ids.append(DstId(rid=rid, pnc=pid))
+    if FUSE:
+        if ids:
+            trs.append(RemoteDMATransfer(dst_ids=ids, dma_engine_mask=m, remote_sem=S["arr%d" % j],
+                                         srcs=[blk], dsts=[blk for _ in ids]))
+            add += len(_engines(m))
+        g.remote_dma_fused(trs, local_sem=S.sent)
+    else:
+        if trs:
+            g.remote_dma_fused(trs, local_sem=S.sent)
+        for i in ids:
+            g.remote_dma(out_ap=blk, in_ap=blk, remote_sem=S["arr%d" % j], local_sem=S.sent, pid=i.pnc, routing_id=i.rid,
+                         dma_engine_mask=m)
+            add += len(_engines(m))
+    return add
+
+
+def rank_program(g, core, T, topo):
+    S, cores, wid = T.sem, T.cores, T.tables["WID"]
+    sites, host, guests, direct, relay, helper, proc = _plan(T, topo)
+    r = T.rank_of(core)
+    if r is None:
+        for j in helper:
+            if helper[j] == core and relay[j]:
+                g.wait_ge(S.fw, len(_engines(topo.mask(cores[j], core) & ~topo.mask(cores[j], cores[relay[j][0]]))))
+                g.wait_ge(S.sent, _spread(g, core, T, topo, j, relay[j], None))
+        return
+    w = wid[r]
+    site = r in sites
+    pe, dve = g.tensor, g.vector
+
+    def slot(j, half):
+        return T.wb[:, (2 * j + half) * D:(2 * j + half + 1) * D]
+
+    def back_masks(s):
+        gs = guests[s]
+        per = 1
+        while per * 2 * len(gs) <= len(_engines(topo.mask(cores[s], cores[gs[0]]))):
+            per *= 2
+        out = []
+        for k, q in enumerate(gs):
+            e = _engines(topo.mask(cores[s], cores[q]))[k * per:(k + 1) * per]
+            out.append(sum(1 << b for b in e))
+        return out
+
+    def load_x(q):
+        q.dma_start(T.xo[:, 0:w], T.x[:, 0:w]).then_inc(S.ldx, 16)
+
+    if not site:
+        load_x(g.sync)
+    if VIA_DRAM:
+        g.scalar.dma_start(T.wd[r, :, 0:D], T.w1[:, :]).then_inc(S.ldd, 16)
+        g.sync.dma_start(T.wd[r, :, D:2 * D], T.w2[:, :]).then_inc(S.ldd, 16)
+    if site or not VIA_DRAM:
+        g.scalar.dma_start(slot(r, 0), T.w1[:, :]).then_inc(S.ldw, 16)
+        g.sync.dma_start(slot(r, 1), T.w2[:, :]).then_inc(S.ldw, 16)
+    if site:
+        load_x(g.scalar)
+
+    sent = 0
+    if not site:
+        h = host[r]
+        off = sum(wid[q] for q in guests[h][:guests[h].index(r)])
+        rid, pid = topo.addr(cores[h], core)
+        m = topo.mask(core, cores[h])
+        g.wait_ge(S.ldx, 16)
+        g.remote_dma(out_ap=T.xg[:, off:off + w], in_ap=T.xo[:, 0:w], remote_sem=S.xga, local_sem=S.sent,
+                     pid=pid, routing_id=rid, dma_engine_mask=m)
+        sent += len(_engines(m))
+
+    if VIA_DRAM:
+        g.wait_ge(S.ldd, 32)
+    else:
+        g.wait_ge(S.ldw, 32)
+    sent += _spread(g, core, T, topo, r, direct[r], helper[r] if HELP and relay[r] else None)
+
+    if not site:
+        k = guests[host[r]].index(r)
+        g.sync.wait_ge(S.yarr, len(_engines(back_masks(host[r])[k])))
+        g.sync.dma_start(T.y[:, 0:w], T.yl[:, 0:w]).then_inc(S.st, 16)
+        g.wait_ge(S.sent, sent)
+        g.wait_ge(S.st, 16)
+        return
+
+    gs = guests[r]
+    gw = sum(wid[q] for q in gs)
+    exps = proc[r]
+    L = len(exps)
+    banks = [T["hp%d" % b] for b in range(NHP)]
+    streams = []
+    if gw:
+        streams.append({"t": "g", "w": gw, "x": T.xg, "sum": T.sg, "hp": banks[NHP // 2:], "h": T.hg, "hw": GW,
+                        "y": T.yg, "xs": (S.xga, sum(len(_engines(topo.mask(cores[q], core))) for q in gs)),
+                        "fin": S.fing, "cp": S.cpg})
+    streams.append({"t": "o", "w": w, "x": T.xo, "sum": T.so, "hp": banks[:NHP // 2] if gw else banks, "h": T.ho,
+                    "hw": TK, "y": T.yo, "xs": (S.ldx, 16), "fin": S.fino, "cp": S.cpo})
+    seen = {}
+
+    def landed(e):
+        src = cores[e] if r in direct[e] else helper[e]
+        return len(_engines(topo.mask(src, core)))
+
+    if VIA_DRAM:
+        for i, e in enumerate(exps[1:]):
+            q = (g.sync, g.scalar)[i % 2]
+            q.wait_ge(S["arr%d" % e], landed(e))
+            q.dma_start(T.wb[:, 2 * e * D:2 * (e + 1) * D], T.wd[e]).then_inc(S["lw%d" % e], 16)
+
+    def mm1(s, i):
+        e = exps[i]
+        if ("w", i) not in seen:
+            seen[("w", i)] = 1
+            if e == r:
+                pe.wait_ge(S.ldw, 32)
+            elif VIA_DRAM:
+                pe.wait_ge(S["lw%d" % e], 16)
+            else:
+                pe.wait_ge(S["arr%d" % e], landed(e))
+        if ("x", s["t"]) not in seen:
+            seen[("x", s["t"])] = 1
+            pe.wait_ge(s["xs"][0], s["xs"][1])
+        nb = len(s["hp"])
+        if i >= nb:
+            pe.wait_ge(S["r%s%d" % (s["t"], i - nb)], 1)
+        pe.matmul(s["hp"][i % nb][:, 0:s["w"]], slot(e, 0), s["x"][:, 0:s["w"]], True, True).then_inc(
+            S["m%s%d" % (s["t"], i)], 1)
+
+    def relu(s, i):
+        dve.wait_ge(S["m%s%d" % (s["t"], i)], 1)
+        dve.tensor_tensor(s["h"][:, i * s["hw"]:i * s["hw"] + s["w"]], s["hp"][i % len(s["hp"])][:, 0:s["w"]],
+                          T.zz[:, 0:s["w"]], AluOpType.max).then_inc(S["r%s%d" % (s["t"], i)], 1)
+
+    def mm2(s, i):
+        pe.wait_ge(S["r%s%d" % (s["t"], i)], 1)
+        mm = pe.matmul(s["sum"][:, 0:s["w"]], slot(exps[i], 1), s["h"][:, i * s["hw"]:i * s["hw"] + s["w"]],
+                       i == 0, i == L - 1)
+        if i == L - 1:
+            mm.then_inc(s["fin"], 1)
+
+    def close(s):
+        dve.wait_ge(s["fin"], 1)
+        dve.tensor_copy(s["y"][:, 0:s["w"]], s["sum"][:, 0:s["w"]]).then_inc(s["cp"], 1)
+
+    dve.memset(T.zz[:, :], 0.0).then_inc(S.zs, 1)
+    dve.wait_ge(S.zs, 1)
+    for s in reversed(streams):
+        mm1(s, 0)
+        relu(s, 0)
+    for i in range(1, L - 1):
+        for s in streams:
+            mm1(s, i)
+            relu(s, i)
+        for s in streams:
+            mm2(s, i - 1)
+    for s in streams:
+        mm1(s, L - 1)
+        relu(s, L - 1)
+        mm2(s, L - 2)
+        mm2(s, L - 1)
+        close(s)
+
+    if gs:
+        masks = back_masks(r)
+        trs = []
+        off = 0
+        for k, q in enumerate(gs):
+            rid, pid = topo.addr(cores[q], core)
+            trs.append(RemoteDMATransfer(dst_ids=[DstId(rid=rid, pnc=pid)], dma_engine_mask=masks[k], remote_sem=S.yarr,
+                                         src=T.yg[:, off:off + wid[q]], dst=T.yl[:, 0:wid[q]]))
+            off += wid[q]
+            sent += len(_engines(masks[k]))
+        g.wait_ge(S.cpg, 1)
+        g.remote_dma_fused(trs, local_sem=S.sent)
+
+    g.sync.wait_ge(S.cpo, 1)
+    g.sync.dma_start(T.y[:, 0:w], T.yo[:, 0:w]).then_inc(S.st, 16)
+    g.wait_ge(S.sent, sent)
+    g.wait_ge(S.st, 16)

@@ -4,285 +4,161 @@ from concourse.mybir import AluOpType
 N = 9
 D = 128
 TK = 512
-GW = 128
 NHP = 6
-
-ALL_SITES = False
-FUSE = True
-HELP = 0
-VIA_DRAM = False
 
 SCRATCH = {
     "wb": ("sbuf", [D, N * 2 * D], "bfloat16"),
     "xo": ("sbuf", [D, TK], "bfloat16"),
-    "xg": ("sbuf", [D, GW], "bfloat16"),
-    "zz": ("sbuf", [D, TK], "float32"),
+    "zz": ("sbuf", [D, TK // 2], "float32"),
     "ho": ("sbuf", [D, N * TK], "bfloat16"),
-    "hg": ("sbuf", [D, N * GW], "bfloat16"),
     "yo": ("sbuf", [D, TK], "bfloat16"),
-    "yg": ("sbuf", [D, GW], "bfloat16"),
-    "yl": ("sbuf", [D, GW], "bfloat16"),
-    "so": ("psum", [D, TK], "float32"),
-    "sg": ("psum", [D, TK], "float32"),
+    "sa": ("psum", [D, TK], "float32"),
+    "sb": ("psum", [D, TK], "float32"),
 }
 for _b in range(NHP):
     SCRATCH["hp%d" % _b] = ("psum", [D, TK], "float32")
-if VIA_DRAM:
-    SCRATCH["wd"] = ("dram", [N, D, 2 * D], "bfloat16")
 
-SEMAPHORES = ["ldw", "ldx", "xga", "zs", "sent", "yarr", "st", "fino", "fing", "cpo", "cpg"]
+SEMAPHORES = ["ldw", "ldx", "zs", "sent", "st", "fina", "finb", "cpa", "cpb"]
 SEMAPHORES += ["arr%d" % _j for _j in range(N)]
-SEMAPHORES += ["m%s%d" % (_s, _j) for _s in "og" for _j in range(N)]
-SEMAPHORES += ["r%s%d" % (_s, _j) for _s in "og" for _j in range(N)]
-if HELP:
-    SEMAPHORES += ["fw"]
-if VIA_DRAM:
-    SEMAPHORES += ["ldd"] + ["lw%d" % _j for _j in range(N)]
+SEMAPHORES += ["m%s%d" % (_s, _j) for _s in "ab" for _j in range(N)]
+SEMAPHORES += ["r%s%d" % (_s, _j) for _s in "ab" for _j in range(N)]
 
 
 def _engines(mask):
     return [b for b in range(16) if (mask >> b) & 1]
 
 
-def _plan(T, topo):
-    wid, cores = T.tables["WID"], T.cores
+def _timetable(cores, wid, topo):
     n = len(cores)
-    wide = [r for r in range(n) if wid[r] > 2 * D]
-    narrow = [r for r in range(n) if r not in wide]
-    load = {s: wid[s] for s in wide}
-    host = {}
-    if not ALL_SITES:
-        for near in (topo.mates, topo.same_plane, lambda a, b: True):
-            for r in narrow:
-                if r in host:
-                    continue
-                cand = [s for s in wide if near(cores[r], cores[s]) and load[s] + wid[r] <= TK
-                        and load[s] - wid[s] + wid[r] <= GW]
-                if cand:
-                    s = min(cand, key=lambda q: (load[q], q))
-                    host[r] = s
-                    load[s] += wid[r]
-    sites = list(range(n)) if ALL_SITES else wide
-    guests = {s: [r for r in narrow if host.get(r) == s] for s in sites}
-    ns = len(wide)
-    free = min(range(ns), key=lambda a: (load[wide[a]] - wid[wide[a]], a))
-    order = {}
-    for j in range(n):
-        k = wide.index(j) + 1 if j in wide else narrow.index(j) + free + 1
-        order[j] = [wide[(k + w) % ns] for w in range(ns) if wide[(k + w) % ns] != j]
-        if ALL_SITES:
-            order[j] += [narrow[(j + w) % len(narrow)] for w in range(len(narrow)) if narrow[(j + w) % len(narrow)] != j]
-    helper = {}
-    if HELP:
-        nsim = topo.CORES_PER_HOST * (1 + max(topo.host(c) for c in cores))
+    turns = n - 1
+    nsim = topo.CORES_PER_HOST * (1 + max(topo.host(c) for c in cores))
+
+    def place(c):
+        return (topo.host(c), topo.chip(c))
+
+    beside = [place(min(c for c in range(nsim) if topo.mates(a, c))) for a in cores]
+    wide = [wid[r] > TK // 2 for r in range(n)]
+    mate = [[topo.mates(cores[a], cores[b]) for b in range(n)] for a in range(n)]
+    port = [[None if mate[a][b] or a == b else place(cores[a]) if topo.same_plane(cores[a], cores[b]) else beside[a]
+             for b in range(n)] for a in range(n)]
+    left = [[d for d in range(n) if d != j] for j in range(n)]
+    plan = [[None] * n for _ in range(turns)]
+
+    def room(t, spare):
+        if any(sum(1 for j in range(n) if d in left[j] and not mate[j][d]) > t for d in range(n)):
+            return False
+        due = {}
         for j in range(n):
-            helper[j] = min(c for c in range(nsim) if topo.host(c) == topo.host(cores[j])
-                            and topo.chip(c) == topo.chip(cores[j]) and topo.die(c) != topo.die(cores[j])
-                            and c not in cores and all(topo.may_write(c, cores[s]) for s in order[j]))
-    direct = {j: order[j][:len(order[j]) - HELP] for j in range(n)}
-    relay = {j: order[j][len(order[j]) - HELP:] for j in range(n)}
+            for d in left[j]:
+                if port[j][d] is not None:
+                    due[port[j][d]] = due.get(port[j][d], 0) + 1
+        return sum(max(0, v - t) for v in due.values()) <= spare
 
-    def due(j, s):
-        return direct[j].index(s) if s in direct[j] else 2 + relay[j].index(s)
-    proc = {}
-    for s in sites:
-        proc[s] = [s] + sorted([j for j in range(n) if j != s], key=lambda j: (due(j, s), j in narrow, j))
-    return sites, host, guests, direct, relay, helper, proc
+    def go(t, j, used, spare):
+        if t < 0:
+            return True
+        if j == n:
+            return room(t, spare) and go(t - 1, 0, [], spare)
+        for d in sorted(left[j], key=lambda q: (wide[q] if 2 * t >= turns else not wide[q], (q - j) % n)):
+            key, out = (mate[j][d], d), ("out", port[j][d])
+            if key in used or (t == turns - 1 and wide[d]):
+                continue
+            twice = 1 if port[j][d] is not None and out in used else 0
+            if twice > spare:
+                continue
+            used.append(key)
+            used.append(out)
+            left[j].remove(d)
+            plan[t][j] = d
+            if go(t, j + 1, used, spare - twice):
+                return True
+            left[j].append(d)
+            used.remove(key)
+            used.remove(out)
+        return False
 
-
-def _spread(g, core, T, topo, j, dsts, extra):
-    S, cores = T.sem, T.cores
-    blk = T.wd[j] if VIA_DRAM else T.wb[:, 2 * j * D:2 * (j + 1) * D]
-    trs, add = [], 0
-    m = 0
-    if dsts:
-        m = topo.mask(core, cores[dsts[0]])
-        for s in dsts:
-            m &= topo.mask(core, cores[s])
-    if extra is not None:
-        rid, pid = topo.addr(extra, core)
-        mx = topo.mask(core, extra) & ~m
-        trs.append(RemoteDMATransfer(dst_ids=[DstId(rid=rid, pnc=pid)], dma_engine_mask=mx, remote_sem=S.fw,
-                                     srcs=[blk], dsts=[blk]))
-        add += len(_engines(mx))
-    ids = []
-    for s in dsts:
-        rid, pid = topo.addr(cores[s], core)
-        ids.append(DstId(rid=rid, pnc=pid))
-    if FUSE:
-        if ids:
-            trs.append(RemoteDMATransfer(dst_ids=ids, dma_engine_mask=m, remote_sem=S["arr%d" % j],
-                                         srcs=[blk], dsts=[blk for _ in ids]))
-            add += len(_engines(m))
-        g.remote_dma_fused(trs, local_sem=S.sent)
-    else:
-        if trs:
-            g.remote_dma_fused(trs, local_sem=S.sent)
-        for i in ids:
-            g.remote_dma(out_ap=blk, in_ap=blk, remote_sem=S["arr%d" % j], local_sem=S.sent, pid=i.pnc, routing_id=i.rid,
-                         dma_engine_mask=m)
-            add += len(_engines(m))
-    return add
+    spare = 0
+    while not go(turns - 1, 0, [], spare):
+        spare += 1
+    return plan
 
 
 def rank_program(g, core, T, topo):
     S, cores, wid = T.sem, T.cores, T.tables["WID"]
-    sites, host, guests, direct, relay, helper, proc = _plan(T, topo)
     r = T.rank_of(core)
     if r is None:
-        for j in helper:
-            if helper[j] == core and relay[j]:
-                g.wait_ge(S.fw, len(_engines(topo.mask(cores[j], core) & ~topo.mask(cores[j], cores[relay[j][0]]))))
-                g.wait_ge(S.sent, _spread(g, core, T, topo, j, relay[j], None))
         return
+    n = len(cores)
     w = wid[r]
-    site = r in sites
     pe, dve = g.tensor, g.vector
+    plan = _timetable(cores, wid, topo)
 
     def slot(j, half):
         return T.wb[:, (2 * j + half) * D:(2 * j + half + 1) * D]
 
-    def back_masks(s):
-        gs = guests[s]
-        per = 1
-        while per * 2 * len(gs) <= len(_engines(topo.mask(cores[s], cores[gs[0]]))):
-            per *= 2
-        out = []
-        for k, q in enumerate(gs):
-            e = _engines(topo.mask(cores[s], cores[q]))[k * per:(k + 1) * per]
-            out.append(sum(1 << b for b in e))
-        return out
+    g.scalar.dma_start(slot(r, 0), T.w1[:, :]).then_inc(S.ldw, 16)
+    g.sync.dma_start(slot(r, 1), T.w2[:, :]).then_inc(S.ldw, 16)
+    g.scalar.dma_start(T.xo[:, 0:w], T.x[:, 0:w]).then_inc(S.ldx, 16)
 
-    def load_x(q):
-        q.dma_start(T.xo[:, 0:w], T.x[:, 0:w]).then_inc(S.ldx, 16)
+    dsts = [row[r] for row in plan]
+    blk = T.wb[:, 2 * r * D:2 * (r + 1) * D]
+    m = topo.mask(core, cores[dsts[0]])
+    ids = []
+    for s in dsts:
+        m &= topo.mask(core, cores[s])
+        rid, pid = topo.addr(cores[s], core)
+        ids.append(DstId(rid=rid, pnc=pid))
+    g.wait_ge(S.ldw, 32)
+    g.remote_dma_fused([RemoteDMATransfer(dst_ids=ids, dma_engine_mask=m, remote_sem=S["arr%d" % r],
+                                          srcs=[blk], dsts=[blk for _ in ids])], local_sem=S.sent)
 
-    if not site:
-        load_x(g.sync)
-    if VIA_DRAM:
-        g.scalar.dma_start(T.wd[r, :, 0:D], T.w1[:, :]).then_inc(S.ldd, 16)
-        g.sync.dma_start(T.wd[r, :, D:2 * D], T.w2[:, :]).then_inc(S.ldd, 16)
-    if site or not VIA_DRAM:
-        g.scalar.dma_start(slot(r, 0), T.w1[:, :]).then_inc(S.ldw, 16)
-        g.sync.dma_start(slot(r, 1), T.w2[:, :]).then_inc(S.ldw, 16)
-    if site:
-        load_x(g.scalar)
-
-    sent = 0
-    if not site:
-        h = host[r]
-        off = sum(wid[q] for q in guests[h][:guests[h].index(r)])
-        rid, pid = topo.addr(cores[h], core)
-        m = topo.mask(core, cores[h])
-        g.wait_ge(S.ldx, 16)
-        g.remote_dma(out_ap=T.xg[:, off:off + w], in_ap=T.xo[:, 0:w], remote_sem=S.xga, local_sem=S.sent,
-                     pid=pid, routing_id=rid, dma_engine_mask=m)
-        sent += len(_engines(m))
-
-    if VIA_DRAM:
-        g.wait_ge(S.ldd, 32)
-    else:
-        g.wait_ge(S.ldw, 32)
-    sent += _spread(g, core, T, topo, r, direct[r], helper[r] if HELP and relay[r] else None)
-
-    if not site:
-        k = guests[host[r]].index(r)
-        g.sync.wait_ge(S.yarr, len(_engines(back_masks(host[r])[k])))
-        g.sync.dma_start(T.y[:, 0:w], T.yl[:, 0:w]).then_inc(S.st, 16)
-        g.wait_ge(S.sent, sent)
-        g.wait_ge(S.st, 16)
-        return
-
-    gs = guests[r]
-    gw = sum(wid[q] for q in gs)
-    exps = proc[r]
+    exps = [r]
+    for row in plan:
+        exps += sorted([j for j in range(n) if row[j] == r], key=lambda j: not topo.mates(cores[j], core))
     L = len(exps)
-    banks = [T["hp%d" % b] for b in range(NHP)]
-    streams = []
-    if gw:
-        streams.append({"t": "g", "w": gw, "x": T.xg, "sum": T.sg, "hp": banks[NHP // 2:], "h": T.hg, "hw": GW,
-                        "y": T.yg, "xs": (S.xga, sum(len(_engines(topo.mask(cores[q], core))) for q in gs)),
-                        "fin": S.fing, "cp": S.cpg})
-    streams.append({"t": "o", "w": w, "x": T.xo, "sum": T.so, "hp": banks[:NHP // 2] if gw else banks, "h": T.ho,
-                    "hw": TK, "y": T.yo, "xs": (S.ldx, 16), "fin": S.fino, "cp": S.cpo})
-    seen = {}
+    cuts = [(0, w // 2), (w // 2, w)] if w > TK // 2 else [(0, w)]
+    ns = len(cuts)
+    nb = NHP // ns
+    sums, fins, cps, qs = (T.sa, T.sb), (S.fina, S.finb), (S.cpa, S.cpb), (g.sync, g.scalar)
 
-    def landed(e):
-        src = cores[e] if r in direct[e] else helper[e]
-        return len(_engines(topo.mask(src, core)))
-
-    if VIA_DRAM:
-        for i, e in enumerate(exps[1:]):
-            q = (g.sync, g.scalar)[i % 2]
-            q.wait_ge(S["arr%d" % e], landed(e))
-            q.dma_start(T.wb[:, 2 * e * D:2 * (e + 1) * D], T.wd[e]).then_inc(S["lw%d" % e], 16)
-
-    def mm1(s, i):
+    def layer1(i):
         e = exps[i]
-        if ("w", i) not in seen:
-            seen[("w", i)] = 1
-            if e == r:
-                pe.wait_ge(S.ldw, 32)
-            elif VIA_DRAM:
-                pe.wait_ge(S["lw%d" % e], 16)
-            else:
-                pe.wait_ge(S["arr%d" % e], landed(e))
-        if ("x", s["t"]) not in seen:
-            seen[("x", s["t"])] = 1
-            pe.wait_ge(s["xs"][0], s["xs"][1])
-        nb = len(s["hp"])
-        if i >= nb:
-            pe.wait_ge(S["r%s%d" % (s["t"], i - nb)], 1)
-        pe.matmul(s["hp"][i % nb][:, 0:s["w"]], slot(e, 0), s["x"][:, 0:s["w"]], True, True).then_inc(
-            S["m%s%d" % (s["t"], i)], 1)
+        if e == r:
+            pe.wait_ge(S.ldw, 32)
+            pe.wait_ge(S.ldx, 16)
+        else:
+            pe.wait_ge(S["arr%d" % e], len(_engines(topo.mask(cores[e], core))))
+        for k, (c0, c1) in enumerate(cuts):
+            tag, bank = "ab"[k], T["hp%d" % (k * nb + i % nb)]
+            if i >= nb:
+                pe.wait_ge(S["r%s%d" % (tag, i - nb)], 1)
+            pe.matmul(bank[:, 0:c1 - c0], slot(e, 0), T.xo[:, c0:c1], True, True).then_inc(S["m%s%d" % (tag, i)], 1)
+            dve.wait_ge(S["m%s%d" % (tag, i)], 1)
+            dve.tensor_tensor(T.ho[:, i * TK + c0:i * TK + c1], bank[:, 0:c1 - c0], T.zz[:, 0:c1 - c0],
+                              AluOpType.max).then_inc(S["r%s%d" % (tag, i)], 1)
 
-    def relu(s, i):
-        dve.wait_ge(S["m%s%d" % (s["t"], i)], 1)
-        dve.tensor_tensor(s["h"][:, i * s["hw"]:i * s["hw"] + s["w"]], s["hp"][i % len(s["hp"])][:, 0:s["w"]],
-                          T.zz[:, 0:s["w"]], AluOpType.max).then_inc(S["r%s%d" % (s["t"], i)], 1)
-
-    def mm2(s, i):
-        pe.wait_ge(S["r%s%d" % (s["t"], i)], 1)
-        mm = pe.matmul(s["sum"][:, 0:s["w"]], slot(exps[i], 1), s["h"][:, i * s["hw"]:i * s["hw"] + s["w"]],
-                       i == 0, i == L - 1)
+    def layer2(k, i):
+        c0, c1 = cuts[k]
+        pe.wait_ge(S["r%s%d" % ("ab"[k], i)], 1)
+        mm = pe.matmul(sums[k][:, 0:c1 - c0], slot(exps[i], 1), T.ho[:, i * TK + c0:i * TK + c1], i == 0, i == L - 1)
         if i == L - 1:
-            mm.then_inc(s["fin"], 1)
-
-    def close(s):
-        dve.wait_ge(s["fin"], 1)
-        dve.tensor_copy(s["y"][:, 0:s["w"]], s["sum"][:, 0:s["w"]]).then_inc(s["cp"], 1)
+            mm.then_inc(fins[k], 1)
 
     dve.memset(T.zz[:, :], 0.0).then_inc(S.zs, 1)
     dve.wait_ge(S.zs, 1)
-    for s in reversed(streams):
-        mm1(s, 0)
-        relu(s, 0)
-    for i in range(1, L - 1):
-        for s in streams:
-            mm1(s, i)
-            relu(s, i)
-        for s in streams:
-            mm2(s, i - 1)
-    for s in streams:
-        mm1(s, L - 1)
-        relu(s, L - 1)
-        mm2(s, L - 2)
-        mm2(s, L - 1)
-        close(s)
+    for i in range(L):
+        layer1(i)
+        if 0 < i < L - 1:
+            for k in range(ns):
+                layer2(k, i - 1)
+    for k in range(ns):
+        c0, c1 = cuts[k]
+        layer2(k, L - 2)
+        layer2(k, L - 1)
+        dve.wait_ge(fins[k], 1)
+        dve.tensor_copy(T.yo[:, c0:c1], sums[k][:, 0:c1 - c0]).then_inc(cps[k], 1)
+        qs[k].wait_ge(cps[k], 1)
+        qs[k].dma_start(T.y[:, c0:c1], T.yo[:, c0:c1]).then_inc(S.st, 16)
 
-    if gs:
-        masks = back_masks(r)
-        trs = []
-        off = 0
-        for k, q in enumerate(gs):
-            rid, pid = topo.addr(cores[q], core)
-            trs.append(RemoteDMATransfer(dst_ids=[DstId(rid=rid, pnc=pid)], dma_engine_mask=masks[k], remote_sem=S.yarr,
-                                         src=T.yg[:, off:off + wid[q]], dst=T.yl[:, 0:wid[q]]))
-            off += wid[q]
-            sent += len(_engines(masks[k]))
-        g.wait_ge(S.cpg, 1)
-        g.remote_dma_fused(trs, local_sem=S.sent)
-
-    g.sync.wait_ge(S.cpo, 1)
-    g.sync.dma_start(T.y[:, 0:w], T.yo[:, 0:w]).then_inc(S.st, 16)
-    g.wait_ge(S.sent, sent)
-    g.wait_ge(S.st, 16)
+    g.wait_ge(S.sent, len(_engines(m)))
+    g.wait_ge(S.st, 16 * ns)

from concourse.bass import DstId, RemoteDMATransfer
from concourse.mybir import AluOpType

N = 9
D = 128
TK = 512
NHP = 6

SCRATCH = {
    "wb": ("sbuf", [D, N * 2 * D], "bfloat16"),
    "xo": ("sbuf", [D, TK], "bfloat16"),
    "zz": ("sbuf", [D, TK // 2], "float32"),
    "ho": ("sbuf", [D, N * TK], "bfloat16"),
    "yo": ("sbuf", [D, TK], "bfloat16"),
    "sa": ("psum", [D, TK], "float32"),
    "sb": ("psum", [D, TK], "float32"),
}
for _b in range(NHP):
    SCRATCH["hp%d" % _b] = ("psum", [D, TK], "float32")

SEMAPHORES = ["ldw", "ldx", "zs", "sent", "st", "fina", "finb", "cpa", "cpb"]
SEMAPHORES += ["arr%d" % _j for _j in range(N)]
SEMAPHORES += ["m%s%d" % (_s, _j) for _s in "ab" for _j in range(N)]
SEMAPHORES += ["r%s%d" % (_s, _j) for _s in "ab" for _j in range(N)]


def _engines(mask):
    return [b for b in range(16) if (mask >> b) & 1]


def _timetable(cores, wid, topo):
    n = len(cores)
    turns = n - 1
    nsim = topo.CORES_PER_HOST * (1 + max(topo.host(c) for c in cores))

    def place(c):
        return (topo.host(c), topo.chip(c))

    beside = [place(min(c for c in range(nsim) if topo.mates(a, c))) for a in cores]
    wide = [wid[r] > TK // 2 for r in range(n)]
    mate = [[topo.mates(cores[a], cores[b]) for b in range(n)] for a in range(n)]
    port = [[None if mate[a][b] or a == b else place(cores[a]) if topo.same_plane(cores[a], cores[b]) else beside[a]
             for b in range(n)] for a in range(n)]
    left = [[d for d in range(n) if d != j] for j in range(n)]
    plan = [[None] * n for _ in range(turns)]

    def room(t, spare):
        if any(sum(1 for j in range(n) if d in left[j] and not mate[j][d]) > t for d in range(n)):
            return False
        due = {}
        for j in range(n):
            for d in left[j]:
                if port[j][d] is not None:
                    due[port[j][d]] = due.get(port[j][d], 0) + 1
        return sum(max(0, v - t) for v in due.values()) <= spare

    def go(t, j, used, spare):
        if t < 0:
            return True
        if j == n:
            return room(t, spare) and go(t - 1, 0, [], spare)
        for d in sorted(left[j], key=lambda q: (wide[q] if 2 * t >= turns else not wide[q], (q - j) % n)):
            key, out = (mate[j][d], d), ("out", port[j][d])
            if key in used or (t == turns - 1 and wide[d]):
                continue
            twice = 1 if port[j][d] is not None and out in used else 0
            if twice > spare:
                continue
            used.append(key)
            used.append(out)
            left[j].remove(d)
            plan[t][j] = d
            if go(t, j + 1, used, spare - twice):
                return True
            left[j].append(d)
            used.remove(key)
            used.remove(out)
        return False

    spare = 0
    while not go(turns - 1, 0, [], spare):
        spare += 1
    return plan


def rank_program(g, core, T, topo):
    S, cores, wid = T.sem, T.cores, T.tables["WID"]
    r = T.rank_of(core)
    if r is None:
        return
    n = len(cores)
    w = wid[r]
    pe, dve = g.tensor, g.vector
    plan = _timetable(cores, wid, topo)

    def slot(j, half):
        return T.wb[:, (2 * j + half) * D:(2 * j + half + 1) * D]

    g.scalar.dma_start(slot(r, 0), T.w1[:, :]).then_inc(S.ldw, 16)
    g.sync.dma_start(slot(r, 1), T.w2[:, :]).then_inc(S.ldw, 16)
    g.scalar.dma_start(T.xo[:, 0:w], T.x[:, 0:w]).then_inc(S.ldx, 16)

    dsts = [row[r] for row in plan]
    blk = T.wb[:, 2 * r * D:2 * (r + 1) * D]
    m = topo.mask(core, cores[dsts[0]])
    ids = []
    for s in dsts:
        m &= topo.mask(core, cores[s])
        rid, pid = topo.addr(cores[s], core)
        ids.append(DstId(rid=rid, pnc=pid))
    g.wait_ge(S.ldw, 32)
    g.remote_dma_fused([RemoteDMATransfer(dst_ids=ids, dma_engine_mask=m, remote_sem=S["arr%d" % r],
                                          srcs=[blk], dsts=[blk for _ in ids])], local_sem=S.sent)

    exps = [r]
    for row in plan:
        exps += sorted([j for j in range(n) if row[j] == r], key=lambda j: not topo.mates(cores[j], core))
    L = len(exps)
    cuts = [(0, w // 2), (w // 2, w)] if w > TK // 2 else [(0, w)]
    ns = len(cuts)
    nb = NHP // ns
    sums, fins, cps, qs = (T.sa, T.sb), (S.fina, S.finb), (S.cpa, S.cpb), (g.sync, g.scalar)

    def layer1(i):
        e = exps[i]
        if e == r:
            pe.wait_ge(S.ldw, 32)
            pe.wait_ge(S.ldx, 16)
        else:
            pe.wait_ge(S["arr%d" % e], len(_engines(topo.mask(cores[e], core))))
        for k, (c0, c1) in enumerate(cuts):
            tag, bank = "ab"[k], T["hp%d" % (k * nb + i % nb)]
            if i >= nb:
                pe.wait_ge(S["r%s%d" % (tag, i - nb)], 1)
            pe.matmul(bank[:, 0:c1 - c0], slot(e, 0), T.xo[:, c0:c1], True, True).then_inc(S["m%s%d" % (tag, i)], 1)
            dve.wait_ge(S["m%s%d" % (tag, i)], 1)
            dve.tensor_tensor(T.ho[:, i * TK + c0:i * TK + c1], bank[:, 0:c1 - c0], T.zz[:, 0:c1 - c0],
                              AluOpType.max).then_inc(S["r%s%d" % (tag, i)], 1)

    def layer2(k, i):
        c0, c1 = cuts[k]
        pe.wait_ge(S["r%s%d" % ("ab"[k], i)], 1)
        mm = pe.matmul(sums[k][:, 0:c1 - c0], slot(exps[i], 1), T.ho[:, i * TK + c0:i * TK + c1], i == 0, i == L - 1)
        if i == L - 1:
            mm.then_inc(fins[k], 1)

    dve.memset(T.zz[:, :], 0.0).then_inc(S.zs, 1)
    dve.wait_ge(S.zs, 1)
    for i in range(L):
        layer1(i)
        if 0 < i < L - 1:
            for k in range(ns):
                layer2(k, i - 1)
    for k in range(ns):
        c0, c1 = cuts[k]
        layer2(k, L - 2)
        layer2(k, L - 1)
        dve.wait_ge(fins[k], 1)
        dve.tensor_copy(T.yo[:, c0:c1], sums[k][:, 0:c1 - c0]).then_inc(cps[k], 1)
        qs[k].wait_ge(cps[k], 1)
        qs[k].dma_start(T.y[:, c0:c1], T.yo[:, c0:c1]).then_inc(S.st, 16)

    g.wait_ge(S.sent, len(_engines(m)))
    g.wait_ge(S.st, 16 * ns)
